import numpy as np
CORES = [68,69,70,71,76,77,78,79,84,85,86,87,92,93,94,95]
N = 16
GROUPS = [[0,1,2,3],[4,5,6,7],[8,9,10,11],[12,13,14,15]]
def setup_inputs(rng):
    return {"x": rng.standard_normal((N, 128, 128), dtype=np.float32)}
def reference(x):
    y = np.empty((N, 128, 128), x.dtype)
    for g in GROUPS:
        n = len(g); b = x.shape[2] // n
        for i, r in enumerate(g):
            y[r] = np.concatenate([x[s][:, i * b:(i + 1) * b] for s in g], axis=1)
    return {"y": y}

@@ -1,0 +1,47 @@
+from concourse.bass import DstId, RemoteDMATransfer
+
+SCRATCH = {
+    "xs": ("sbuf", [128, 128], "float32"),
+    "land": ("sbuf", [128, 128], "float32"),
+}
+SEMAPHORES = ["loaded", "arrived", "sent", "stored"]
+
+
+def rank_program(g, core, T, topo):
+    rank = T.rank_of(core)
+    if rank is None:
+        return
+    group = [grp for grp in T.tables["GROUPS"] if rank in grp][0]
+    n = len(group)
+    i = group.index(rank)
+    b = T.x.shape[1] // n
+
+    def blk(t, k):
+        return t[:, k * b:(k + 1) * b]
+
+    eng = 16
+    while eng * (n - 1) > 16:
+        eng //= 2
+
+    g.sync.dma_start(T.xs[:], T.x[:]).then_inc(T.sem.loaded, 16)
+    g.sync.dma_start(blk(T.land, i), blk(T.x, i)).then_inc(T.sem.arrived, 16)
+
+    g.wait_ge(T.sem.loaded, 16)
+    transfers = []
+    for k in range(1, n):
+        j = (i + k) % n
+        rid, pid, _se = topo.addr(T.cores[group[j]])
+        transfers.append(RemoteDMATransfer(
+            dst_ids=[DstId(rid=rid, pnc=pid)],
+            dma_engine_mask=((1 << eng) - 1) << ((k - 1) * eng),
+            remote_sem=T.sem.arrived,
+            src=blk(T.xs, j),
+            dst=blk(T.land, i),
+        ))
+    g.remote_dma_fused(transfers, local_sem=T.sem.sent)
+
+    g.sync.wait_ge(T.sem.arrived, (n - 1) * eng + 16)
+    g.sync.dma_start(T.y[:], T.land[:]).then_inc(T.sem.stored, 16)
+
+    g.wait_ge(T.sem.sent, (n - 1) * eng)
+    g.sync.wait_ge(T.sem.stored, 16)

@@ -19,29 +19,28 @@ def rank_program(g, core, T, topo):
     def blk(t, k):
         return t[:, k * b:(k + 1) * b]
 
-    eng = 16
-    while eng * (n - 1) > 16:
-        eng //= 2
-
     g.sync.dma_start(T.xs[:], T.x[:]).then_inc(T.sem.loaded, 16)
     g.sync.dma_start(blk(T.land, i), blk(T.x, i)).then_inc(T.sem.arrived, 16)
 
     g.wait_ge(T.sem.loaded, 16)
     transfers = []
-    for k in range(1, n):
+    for k in (1, 2):
         j = (i + k) % n
         rid, pid, _se = topo.addr(T.cores[group[j]])
         transfers.append(RemoteDMATransfer(
             dst_ids=[DstId(rid=rid, pnc=pid)],
-            dma_engine_mask=((1 << eng) - 1) << ((k - 1) * eng),
+            dma_engine_mask=0xFF << ((k - 1) * 8),
             remote_sem=T.sem.arrived,
             src=blk(T.xs, j),
             dst=blk(T.land, i),
         ))
     g.remote_dma_fused(transfers, local_sem=T.sem.sent)
+    j = (i + 3) % n
+    rid, pid, _se = topo.addr(T.cores[group[j]])
+    g.remote_dma(blk(T.land, i), blk(T.xs, j), T.sem.arrived, T.sem.sent, pid, rid, 0xFFFF)
 
-    g.sync.wait_ge(T.sem.arrived, (n - 1) * eng + 16)
+    g.sync.wait_ge(T.sem.arrived, 32 + 16)
     g.sync.dma_start(T.y[:], T.land[:]).then_inc(T.sem.stored, 16)
 
-    g.wait_ge(T.sem.sent, (n - 1) * eng)
+    g.wait_ge(T.sem.sent, 32)
     g.sync.wait_ge(T.sem.stored, 16)

@@ -4,7 +4,7 @@ SCRATCH = {
     "xs": ("sbuf", [128, 128], "float32"),
     "land": ("sbuf", [128, 128], "float32"),
 }
-SEMAPHORES = ["loaded", "arrived", "sent", "stored"]
+SEMAPHORES = ["loaded1", "loaded2", "far", "near", "sent", "stored"]
 
 
 def rank_program(g, core, T, topo):
@@ -13,34 +13,41 @@ def rank_program(g, core, T, topo):
         return
     group = [grp for grp in T.tables["GROUPS"] if rank in grp][0]
     n = len(group)
+    assert n == 4
     i = group.index(rank)
     b = T.x.shape[1] // n
+    nb = i ^ 1
+    f0 = 2 - 2 * (i // 2)
 
-    def blk(t, k):
-        return t[:, k * b:(k + 1) * b]
+    def cols(t, k, m=1):
+        return t[:, k * b:(k + m) * b]
 
-    g.sync.dma_start(T.xs[:], T.x[:]).then_inc(T.sem.loaded, 16)
-    g.sync.dma_start(blk(T.land, i), blk(T.x, i)).then_inc(T.sem.arrived, 16)
+    g.sync.dma_start(cols(T.xs, f0, 2), cols(T.x, f0, 2)).then_inc(T.sem.loaded1, 16)
+    g.sync.dma_start(cols(T.xs, nb), cols(T.x, nb)).then_inc(T.sem.loaded2, 16)
+    g.sync.dma_start(cols(T.y, i), cols(T.x, i)).then_inc(T.sem.stored, 16)
 
-    g.wait_ge(T.sem.loaded, 16)
+    g.wait_ge(T.sem.loaded1, 16)
     transfers = []
-    for k in (1, 2):
-        j = (i + k) % n
+    for k in range(2):
+        j = f0 + ((i + k) & 1)
         rid, pid, _se = topo.addr(T.cores[group[j]])
         transfers.append(RemoteDMATransfer(
             dst_ids=[DstId(rid=rid, pnc=pid)],
-            dma_engine_mask=0xFF << ((k - 1) * 8),
-            remote_sem=T.sem.arrived,
-            src=blk(T.xs, j),
-            dst=blk(T.land, i),
+            dma_engine_mask=0xFF << (k * 8),
+            remote_sem=T.sem.far,
+            src=cols(T.xs, j),
+            dst=cols(T.land, i),
         ))
     g.remote_dma_fused(transfers, local_sem=T.sem.sent)
-    j = (i + 3) % n
-    rid, pid, _se = topo.addr(T.cores[group[j]])
-    g.remote_dma(blk(T.land, i), blk(T.xs, j), T.sem.arrived, T.sem.sent, pid, rid, 0xFFFF)
+    g.wait_ge(T.sem.loaded2, 16)
+    rid, pid, _se = topo.addr(T.cores[group[nb]])
+    g.remote_dma(cols(T.land, i), cols(T.xs, nb), T.sem.near, T.sem.sent, pid, rid, 0xFFFF)
 
-    g.sync.wait_ge(T.sem.arrived, 32 + 16)
-    g.sync.dma_start(T.y[:], T.land[:]).then_inc(T.sem.stored, 16)
+    g.scalar.wait_ge(T.sem.far, 16)
+    g.scalar.dma_start(cols(T.y, f0, 2), cols(T.land, f0, 2)).then_inc(T.sem.stored, 16)
+
+    g.sync.wait_ge(T.sem.near, 16)
+    g.sync.dma_start(cols(T.y, nb), cols(T.land, nb)).then_inc(T.sem.stored, 16)
 
     g.wait_ge(T.sem.sent, 32)
-    g.sync.wait_ge(T.sem.stored, 16)
+    g.wait_ge(T.sem.stored, 48)

@@ -1,10 +1,8 @@
-from concourse.bass import DstId, RemoteDMATransfer
-
 SCRATCH = {
-    "xs": ("sbuf", [128, 128], "float32"),
-    "land": ("sbuf", [128, 128], "float32"),
+    "stage": ("dram", [4, 128, 32], "float32"),
+    "landd": ("dram", [4, 128, 32], "float32"),
 }
-SEMAPHORES = ["loaded1", "loaded2", "far", "near", "sent", "stored"]
+SEMAPHORES = ["ld1", "ld2", "ld3", "ar1", "ar2", "ar3", "sent", "stored"]
 
 
 def rank_program(g, core, T, topo):
@@ -16,38 +14,26 @@ def rank_program(g, core, T, topo):
     assert n == 4
     i = group.index(rank)
     b = T.x.shape[1] // n
-    nb = i ^ 1
-    f0 = 2 - 2 * (i // 2)
 
-    def cols(t, k, m=1):
-        return t[:, k * b:(k + m) * b]
+    def blk(t, k):
+        return t[:, k * b:(k + 1) * b]
 
-    g.sync.dma_start(cols(T.xs, f0, 2), cols(T.x, f0, 2)).then_inc(T.sem.loaded1, 16)
-    g.sync.dma_start(cols(T.xs, nb), cols(T.x, nb)).then_inc(T.sem.loaded2, 16)
-    g.sync.dma_start(cols(T.y, i), cols(T.x, i)).then_inc(T.sem.stored, 16)
+    for k in range(1, n):
+        g.sync.dma_start(T.stage[k], blk(T.x, (i + k) % n)).then_inc(T.sem["ld%d" % k], 16)
 
-    g.wait_ge(T.sem.loaded1, 16)
-    transfers = []
-    for k in range(2):
-        j = f0 + ((i + k) & 1)
-        rid, pid, _se = topo.addr(T.cores[group[j]])
-        transfers.append(RemoteDMATransfer(
-            dst_ids=[DstId(rid=rid, pnc=pid)],
-            dma_engine_mask=0xFF << (k * 8),
-            remote_sem=T.sem.far,
-            src=cols(T.xs, j),
-            dst=cols(T.land, i),
-        ))
-    g.remote_dma_fused(transfers, local_sem=T.sem.sent)
-    g.wait_ge(T.sem.loaded2, 16)
-    rid, pid, _se = topo.addr(T.cores[group[nb]])
-    g.remote_dma(cols(T.land, i), cols(T.xs, nb), T.sem.near, T.sem.sent, pid, rid, 0xFFFF)
+    for k in range(1, n):
+        rid, pid, _se = topo.addr(T.cores[group[(i + k) % n]])
+        g.wait_ge(T.sem["ld%d" % k], 16)
+        g.remote_dma(T.landd[i], T.stage[k], T.sem["ar%d" % k], T.sem.sent, pid, rid, 0xFFFF)
 
-    g.scalar.wait_ge(T.sem.far, 16)
-    g.scalar.dma_start(cols(T.y, f0, 2), cols(T.land, f0, 2)).then_inc(T.sem.stored, 16)
+    g.scalar.wait_ge(T.sem.ld2, 16)
+    g.scalar.dma_start(blk(T.y, i), blk(T.x, i)).then_inc(T.sem.stored, 16)
 
-    g.sync.wait_ge(T.sem.near, 16)
-    g.sync.dma_start(cols(T.y, nb), cols(T.land, nb)).then_inc(T.sem.stored, 16)
+    for k in range(1, n):
+        q = g.sync if k == 2 else g.scalar
+        j = (i - k) % n
+        q.wait_ge(T.sem["ar%d" % k], 16)
+        q.dma_start(blk(T.y, j), T.landd[j]).then_inc(T.sem.stored, 16)
 
-    g.wait_ge(T.sem.sent, 32)
-    g.wait_ge(T.sem.stored, 48)
+    g.wait_ge(T.sem.sent, 16 * (n - 1))
+    g.wait_ge(T.sem.stored, 16 * n)

SCRATCH = {
    "stage": ("dram", [4, 128, 32], "float32"),
    "landd": ("dram", [4, 128, 32], "float32"),
}
SEMAPHORES = ["ld1", "ld2", "ld3", "ar1", "ar2", "ar3", "sent", "stored"]


def rank_program(g, core, T, topo):
    rank = T.rank_of(core)
    if rank is None:
        return
    group = [grp for grp in T.tables["GROUPS"] if rank in grp][0]
    n = len(group)
    assert n == 4
    i = group.index(rank)
    b = T.x.shape[1] // n

    def blk(t, k):
        return t[:, k * b:(k + 1) * b]

    for k in range(1, n):
        g.sync.dma_start(T.stage[k], blk(T.x, (i + k) % n)).then_inc(T.sem["ld%d" % k], 16)

    for k in range(1, n):
        rid, pid, _se = topo.addr(T.cores[group[(i + k) % n]])
        g.wait_ge(T.sem["ld%d" % k], 16)
        g.remote_dma(T.landd[i], T.stage[k], T.sem["ar%d" % k], T.sem.sent, pid, rid, 0xFFFF)

    g.scalar.wait_ge(T.sem.ld2, 16)
    g.scalar.dma_start(blk(T.y, i), blk(T.x, i)).then_inc(T.sem.stored, 16)

    for k in range(1, n):
        q = g.sync if k == 2 else g.scalar
        j = (i - k) % n
        q.wait_ge(T.sem["ar%d" % k], 16)
        q.dma_start(blk(T.y, j), T.landd[j]).then_inc(T.sem.stored, 16)

    g.wait_ge(T.sem.sent, 16 * (n - 1))
    g.wait_ge(T.sem.stored, 16 * n)
